import numpy as np
import ml_dtypes

BF16 = ml_dtypes.bfloat16


def bf(x):
    return np.asarray(x, np.float32).astype(BF16)


def f32(x):
    return np.asarray(x, np.float32)


def f64(x):
    return np.asarray(x).astype(np.float64)


def striped(idx):
    return np.tile(idx.reshape(-1, 16).T, (8, 1))


def rows(idx, k):
    return np.tile(idx, (k, 1))


def look(tab, idx):
    return np.take_along_axis(f64(tab), rows(idx, len(tab)), axis=1)


K, S, D, V, N, M = 256, 2048, 3, 512, 1536, 512


def setup_inputs():
    return {"tab": f32(np.random.standard_normal((K, S))), "x0": f32(np.random.standard_normal((K, V))), "w": bf(np.random.standard_normal((K, M)) / np.sqrt(K)), "offs": striped(np.random.permutation(S)[:N])}


def reference(tab, x0, w, offs):
    idx = offs[:16].T.reshape(-1)
    x = f64(x0)
    for d in range(D):
        x = np.maximum(x, look(tab, idx[d * V:(d + 1) * V]))
    y = f64(w).T @ x
    return y

@@ -1,0 +1,63 @@
+import concourse.mybir as mybir
+
+F32, BF16, U16 = mybir.dt.float32, mybir.dt.bfloat16, mybir.dt.uint16
+MAX = mybir.AluOpType.max
+
+P = 128
+R, S = 256, 2048
+V, D, M = 512, 3, 512
+BLOCKS = R // P
+M_BLOCKS = M // P
+ENTRIES = 16
+
+FLOPS = 2 * R * M * V + D * R * V
+
+
+def tile_lookup_pool_max_none_kernel(tc, tab, x0, w, offs, out):
+    nc = tc.nc
+    with (
+        tc.tile_pool(name="lists", bufs=1) as lists,
+        tc.tile_pool(name="held", bufs=1) as held,
+        tc.psum_pool(name="psum", bufs=1) as psum,
+    ):
+        offsets = lists.tile([P, D * V // ENTRIES], U16, name="offsets")
+        nc.sync.dma_start(offsets[:], offs)
+
+        windows, centres = [], []
+        for b in range(BLOCKS):
+            rows = slice(b * P, (b + 1) * P)
+            centre = held.tile([P, V], F32, name=f"centre{b}")
+            nc.sync.dma_start(centre[:], x0[rows, :])
+            window = held.tile([P, S], F32, name=f"window{b}")
+            nc.sync.dma_start(window[:], tab[rows, :])
+            centres.append(centre)
+            windows.append(window)
+        weights = held.tile([P, BLOCKS, M], BF16, name="weights")
+        nc.sync.dma_start(weights[:], w.rearrange("(b p) m -> p b m", p=P))
+
+        products = [psum.tile([P, V], F32, name=f"product{m}") for m in range(M_BLOCKS)]
+        for b in range(BLOCKS):
+            largest = centres[b]
+            for d in range(D):
+                larger = held.tile([P, V], F32, name=f"largest{b}_{d}")
+                neighbours = offsets[:, d * V // ENTRIES : (d + 1) * V // ENTRIES]
+                nc.vector.tensor_tensor(larger[:], windows[b][:].indirect(neighbours), largest[:], MAX)
+                largest = larger
+            x = held.tile([P, V], BF16, name=f"x{b}")
+            nc.scalar.copy(x[:], largest[:])
+            for m in range(M_BLOCKS):
+                nc.tensor.matmul(
+                    products[m][:],
+                    weights[:, b, m * P : (m + 1) * P],
+                    x[:],
+                    start=(b == 0),
+                    stop=(b == BLOCKS - 1),
+                )
+
+        for m in range(M_BLOCKS):
+            result = held.tile([P, V], F32, name=f"result{m}")
+            if m % 2 == 0:
+                nc.scalar.copy(result[:], products[m][:])
+            else:
+                nc.vector.tensor_copy(result[:], products[m][:])
+            nc.sync.dma_start(out[m * P : (m + 1) * P, :], result[:])

@@ -9,6 +9,7 @@ V, D, M = 512, 3, 512
 BLOCKS = R // P
 M_BLOCKS = M // P
 ENTRIES = 16
+HALF = V // 2
 
 FLOPS = 2 * R * M * V + D * R * V
 
@@ -35,29 +36,46 @@ def tile_lookup_pool_max_none_kernel(tc, tab, x0, w, offs, out):
         weights = held.tile([P, BLOCKS, M], BF16, name="weights")
         nc.sync.dma_start(weights[:], w.rearrange("(b p) m -> p b m", p=P))
 
-        products = [psum.tile([P, V], F32, name=f"product{m}") for m in range(M_BLOCKS)]
-        for b in range(BLOCKS):
-            largest = centres[b]
+        def pool(b, start, stop):
+            largest = centres[b][:, start:stop]
             for d in range(D):
-                larger = held.tile([P, V], F32, name=f"largest{b}_{d}")
-                neighbours = offsets[:, d * V // ENTRIES : (d + 1) * V // ENTRIES]
-                nc.vector.tensor_tensor(larger[:], windows[b][:].indirect(neighbours), largest[:], MAX)
-                largest = larger
-            x = held.tile([P, V], BF16, name=f"x{b}")
-            nc.scalar.copy(x[:], largest[:])
+                larger = held.tile([P, stop - start], F32, name=f"largest{b}_{start}_{d}")
+                neighbours = offsets[:, (d * V + start) // ENTRIES : (d * V + stop) // ENTRIES]
+                nc.vector.tensor_tensor(larger[:], windows[b][:].indirect(neighbours), largest, MAX)
+                largest = larger[:]
+            return largest
+
+        products = [[psum.tile([P, HALF], F32, name=f"product{h}_{m}") for m in range(M_BLOCKS)] for h in range(2)]
+
+        x = held.tile([P, V], BF16, name="x0_rounded")
+        nc.scalar.copy(x[:], pool(0, 0, V))
+        for h in range(2):
             for m in range(M_BLOCKS):
                 nc.tensor.matmul(
-                    products[m][:],
-                    weights[:, b, m * P : (m + 1) * P],
-                    x[:],
-                    start=(b == 0),
-                    stop=(b == BLOCKS - 1),
+                    products[h][m][:],
+                    weights[:, 0, m * P : (m + 1) * P],
+                    x[:, h * HALF : (h + 1) * HALF],
+                    start=True,
+                    stop=False,
                 )
 
-        for m in range(M_BLOCKS):
-            result = held.tile([P, V], F32, name=f"result{m}")
-            if m % 2 == 0:
-                nc.scalar.copy(result[:], products[m][:])
+        for h in range(2):
+            columns = slice(h * HALF, (h + 1) * HALF)
+            x = held.tile([P, HALF], BF16, name=f"x1_{h}_rounded")
+            largest = pool(1, columns.start, columns.stop)
+            if h == 0:
+                nc.scalar.copy(x[:], largest)
             else:
-                nc.vector.tensor_copy(result[:], products[m][:])
-            nc.sync.dma_start(out[m * P : (m + 1) * P, :], result[:])
+                nc.vector.tensor_copy(x[:], largest)
+            result = held.tile([P, M_BLOCKS, HALF], F32, name=f"result{h}")
+            for m in range(M_BLOCKS):
+                nc.tensor.matmul(products[h][m][:], weights[:, 1, m * P : (m + 1) * P], x[:], start=False, stop=True)
+                if h == 0 or m % 2 == 0:
+                    nc.scalar.copy(result[:, m, :], products[h][m][:])
+                else:
+                    nc.vector.tensor_copy(result[:, m, :], products[h][m][:])
+                if m % 2 == 1:
+                    nc.sync.dma_start(
+                        out[(m - 1) * P : (m + 1) * P, columns].rearrange("(q p) j -> p q j", p=P),
+                        result[:, m - 1 : m + 1, :],
+                    )

@@ -36,46 +36,47 @@ def tile_lookup_pool_max_none_kernel(tc, tab, x0, w, offs, out):
         weights = held.tile([P, BLOCKS, M], BF16, name="weights")
         nc.sync.dma_start(weights[:], w.rearrange("(b p) m -> p b m", p=P))
 
-        def pool(b, start, stop):
-            largest = centres[b][:, start:stop]
-            for d in range(D):
-                larger = held.tile([P, stop - start], F32, name=f"largest{b}_{start}_{d}")
-                neighbours = offsets[:, (d * V + start) // ENTRIES : (d * V + stop) // ENTRIES]
-                nc.vector.tensor_tensor(larger[:], windows[b][:].indirect(neighbours), largest, MAX)
-                largest = larger[:]
-            return largest
-
         products = [[psum.tile([P, HALF], F32, name=f"product{h}_{m}") for m in range(M_BLOCKS)] for h in range(2)]
 
+        halves = [slice(h * HALF, (h + 1) * HALF) for h in range(2)]
+
+        def pool(b):
+            pooled = held.tile([P, V], F32, name=f"pooled{b}")
+            for h, columns in enumerate(halves):
+                largest = centres[b][:, columns]
+                for d in range(D):
+                    first = (d * V + columns.start) // ENTRIES
+                    neighbours = offsets[:, first : first + HALF // ENTRIES]
+                    if d == D - 1:
+                        larger = pooled[:, columns]
+                    else:
+                        partial = held.tile([P, HALF], F32, name=f"partial{b}_{h}_{d}")
+                        larger = partial[:]
+                    nc.vector.tensor_tensor(larger, windows[b][:].indirect(neighbours), largest, MAX)
+                    largest = larger
+            return pooled
+
+        pooled = pool(0)
         x = held.tile([P, V], BF16, name="x0_rounded")
-        nc.scalar.copy(x[:], pool(0, 0, V))
-        for h in range(2):
+        nc.scalar.copy(x[:], pooled[:])
+        for h, columns in enumerate(halves):
             for m in range(M_BLOCKS):
                 nc.tensor.matmul(
-                    products[h][m][:],
-                    weights[:, 0, m * P : (m + 1) * P],
-                    x[:, h * HALF : (h + 1) * HALF],
-                    start=True,
-                    stop=False,
+                    products[h][m][:], weights[:, 0, m * P : (m + 1) * P], x[:, columns], start=True, stop=False
                 )
 
-        for h in range(2):
-            columns = slice(h * HALF, (h + 1) * HALF)
-            x = held.tile([P, HALF], BF16, name=f"x1_{h}_rounded")
-            largest = pool(1, columns.start, columns.stop)
-            if h == 0:
-                nc.scalar.copy(x[:], largest)
-            else:
-                nc.vector.tensor_copy(x[:], largest)
-            result = held.tile([P, M_BLOCKS, HALF], F32, name=f"result{h}")
+        pooled = pool(1)
+        x = held.tile([P, V], BF16, name="x1_rounded")
+        nc.scalar.copy(x[:, halves[0]], pooled[:, halves[0]])
+        nc.vector.tensor_copy(x[:, halves[1]], pooled[:, halves[1]])
+        for h, columns in enumerate(halves):
             for m in range(M_BLOCKS):
-                nc.tensor.matmul(products[h][m][:], weights[:, 1, m * P : (m + 1) * P], x[:], start=False, stop=True)
-                if h == 0 or m % 2 == 0:
-                    nc.scalar.copy(result[:, m, :], products[h][m][:])
+                nc.tensor.matmul(
+                    products[h][m][:], weights[:, 1, m * P : (m + 1) * P], x[:, columns], start=False, stop=True
+                )
+                result = held.tile([P, HALF], F32, name=f"result{h}_{m}")
+                if m % 2 == 0:
+                    nc.scalar.copy(result[:], products[h][m][:])
                 else:
-                    nc.vector.tensor_copy(result[:, m, :], products[h][m][:])
-                if m % 2 == 1:
-                    nc.sync.dma_start(
-                        out[(m - 1) * P : (m + 1) * P, columns].rearrange("(q p) j -> p q j", p=P),
-                        result[:, m - 1 : m + 1, :],
-                    )
+                    nc.vector.tensor_copy(result[:], products[h][m][:])
+                nc.sync.dma_start(out[m * P : (m + 1) * P, columns], result[:])

import concourse.mybir as mybir

F32, BF16, U16 = mybir.dt.float32, mybir.dt.bfloat16, mybir.dt.uint16
MAX = mybir.AluOpType.max

P = 128
R, S = 256, 2048
V, D, M = 512, 3, 512
BLOCKS = R // P
M_BLOCKS = M // P
ENTRIES = 16
HALF = V // 2

FLOPS = 2 * R * M * V + D * R * V


def tile_lookup_pool_max_none_kernel(tc, tab, x0, w, offs, out):
    nc = tc.nc
    with (
        tc.tile_pool(name="lists", bufs=1) as lists,
        tc.tile_pool(name="held", bufs=1) as held,
        tc.psum_pool(name="psum", bufs=1) as psum,
    ):
        offsets = lists.tile([P, D * V // ENTRIES], U16, name="offsets")
        nc.sync.dma_start(offsets[:], offs)

        windows, centres = [], []
        for b in range(BLOCKS):
            rows = slice(b * P, (b + 1) * P)
            centre = held.tile([P, V], F32, name=f"centre{b}")
            nc.sync.dma_start(centre[:], x0[rows, :])
            window = held.tile([P, S], F32, name=f"window{b}")
            nc.sync.dma_start(window[:], tab[rows, :])
            centres.append(centre)
            windows.append(window)
        weights = held.tile([P, BLOCKS, M], BF16, name="weights")
        nc.sync.dma_start(weights[:], w.rearrange("(b p) m -> p b m", p=P))

        products = [[psum.tile([P, HALF], F32, name=f"product{h}_{m}") for m in range(M_BLOCKS)] for h in range(2)]

        halves = [slice(h * HALF, (h + 1) * HALF) for h in range(2)]

        def pool(b):
            pooled = held.tile([P, V], F32, name=f"pooled{b}")
            for h, columns in enumerate(halves):
                largest = centres[b][:, columns]
                for d in range(D):
                    first = (d * V + columns.start) // ENTRIES
                    neighbours = offsets[:, first : first + HALF // ENTRIES]
                    if d == D - 1:
                        larger = pooled[:, columns]
                    else:
                        partial = held.tile([P, HALF], F32, name=f"partial{b}_{h}_{d}")
                        larger = partial[:]
                    nc.vector.tensor_tensor(larger, windows[b][:].indirect(neighbours), largest, MAX)
                    largest = larger
            return pooled

        pooled = pool(0)
        x = held.tile([P, V], BF16, name="x0_rounded")
        nc.scalar.copy(x[:], pooled[:])
        for h, columns in enumerate(halves):
            for m in range(M_BLOCKS):
                nc.tensor.matmul(
                    products[h][m][:], weights[:, 0, m * P : (m + 1) * P], x[:, columns], start=True, stop=False
                )

        pooled = pool(1)
        x = held.tile([P, V], BF16, name="x1_rounded")
        nc.scalar.copy(x[:, halves[0]], pooled[:, halves[0]])
        nc.vector.tensor_copy(x[:, halves[1]], pooled[:, halves[1]])
        for h, columns in enumerate(halves):
            for m in range(M_BLOCKS):
                nc.tensor.matmul(
                    products[h][m][:], weights[:, 1, m * P : (m + 1) * P], x[:, columns], start=False, stop=True
                )
                result = held.tile([P, HALF], F32, name=f"result{h}_{m}")
                if m % 2 == 0:
                    nc.scalar.copy(result[:], products[h][m][:])
                else:
                    nc.vector.tensor_copy(result[:], products[h][m][:])
                nc.sync.dma_start(out[m * P : (m + 1) * P, columns], result[:])
